import numpy as np
import ml_dtypes


def mxq(x, axis, fmt="e4m3"):
    dtype, down = {"e4m3": (ml_dtypes.float8_e4m3fn, 7), "e5m2": (ml_dtypes.float8_e5m2, 14)}[fmt]
    v = np.moveaxis(np.asarray(x, np.float32).astype(ml_dtypes.bfloat16).astype(np.float64), axis, -1)
    blocks = v.reshape(v.shape[:-1] + (-1, 32))
    amax = np.abs(blocks).max(-1, keepdims=True)
    byte = np.maximum(np.where(amax > 0, np.frexp(amax)[1] - 1 + 127, 0) - down, 1)
    scale = np.exp2(byte - 127.0)
    codes = (blocks / scale).astype(np.float32).astype(dtype).astype(np.float64)
    return np.moveaxis((codes * scale).reshape(v.shape), -1, axis)


WIDE = False


def mx_kscale(k):
    if not WIDE:
        return np.ones(k)
    levels = np.array([10, -10, 5, -5, 0])
    if k % 512:
        return np.exp2(np.random.permutation(np.resize(levels, k // 32))).repeat(32)
    a = np.empty((k // 512, 16))
    for p in range(k // 512):
        a[p, :8] = np.random.permutation(np.resize(levels, 8))
        for g in range(8):
            far = levels[np.abs(levels - a[p, g]) >= 10]
            a[p, g + 8] = far[np.random.randint(len(far))]
    return np.exp2(a.ravel()).repeat(32)


def f64(x):
    return np.asarray(x).astype(np.float64)


def striped(idx):
    return np.tile(idx.reshape(-1, 16).T, (8, 1)).astype(np.uint16)


def unstriped(offs):
    return offs[:16].T.reshape(-1).astype(np.int64)


def striped8(idx):
    return np.concatenate([x.reshape(-1, 16).T for x in idx]).astype(np.uint16)


def runs(offs, k):
    lists = np.stack([offs[16 * r : 16 * r + 16].T.reshape(-1) for r in range(8)]).astype(np.int64)
    return lists[np.arange(k) % 512 // 64]


def pack_weight(w):
    k, n = w.shape
    w = f64(np.asarray(w, np.float32).astype(ml_dtypes.bfloat16)).reshape(k // 32, 32, n)
    amax = np.abs(w).max(1)
    byte = np.clip(np.where(amax > 0, np.frexp(amax)[1] - 1 + 127 - 7, 1), 1, 254)
    scaled = (w * np.exp2(127.0 - byte)[:, None, :]).reshape(k, n).astype(np.float32)
    words = np.ascontiguousarray(scaled.reshape(k // 512, 128, 4, n).transpose(0, 1, 3, 2)).astype(ml_dtypes.float8_e4m3fn).view(np.uint8)
    return words, np.ascontiguousarray(byte.astype(np.uint8).reshape(k // 512, 16, n))


def unpack_weight(words, scales):
    g, p, n, _ = words.shape
    vals = np.ascontiguousarray(words).view(ml_dtypes.float8_e4m3fn).astype(np.float64) * np.repeat(np.exp2(scales.astype(np.float64) - 127.0), 8, axis=1)[..., None]
    return vals.transpose(0, 1, 3, 2).reshape(g * 512, n)


K, T, S, V, G, H = 512, 2048, 512, 256, 2048, 512


def setup_inputs():
    n = np.random.standard_normal
    s = mx_kscale(K)[:, None]
    packed_xT = pack_weight(n((K, T)) * s)
    packed_dT = pack_weight(n((K, G)) / s)
    perm = np.stack([np.random.permutation(S) for _ in range(8)])
    return {
        "x_words": packed_xT[0],
        "x_scales": packed_xT[1],
        "d_words": packed_dT[0],
        "d_scales": packed_dT[1],
        "gs": (np.random.uniform(0.5, 1.5, (K, 1)) * s).astype(np.float32),
        "offs": striped(np.random.permutation(T)[:S]),
        "k1": striped8(np.random.randint(0, G, (8, H))),
        "la": striped8(perm[:, :V]),
        "lb": striped8(perm[:, V:]),
        "k2": striped8(np.random.randint(0, G, (8, H))),
    }


def reference(x_words, x_scales, d_words, d_scales, gs, offs, k1, la, lb, k2):
    d_k2 = unpack_weight(d_words, d_scales)[np.arange(K)[:, None], runs(k2, K)]
    d_k1 = unpack_weight(d_words, d_scales)[np.arange(K)[:, None], runs(k1, K)]
    xq = unpack_weight(x_words, x_scales)[:, unstriped(offs)]
    h = 0.0625 * (d_k1.T @ xq)
    p = h[np.arange(H)[:, None], runs(la, H)]
    qv = h[np.arange(H)[:, None], runs(lb, H)]
    lo = np.minimum(p, qv)
    hi = np.maximum(p, qv)
    d1 = np.zeros((H, S))
    d1[np.arange(H)[:, None], runs(la, H)] = hi
    d2 = d1.copy()
    d2[np.arange(H)[:, None], runs(lb, H)] = lo
    z = f64(gs) * d2
    return 0.0625 * ((d_k2.T @ mxq(z, 0, "e4m3")))

@@ -1,0 +1,163 @@
+from contextlib import ExitStack
+
+import concourse.mybir as mybir
+
+K, T, S, V, G, H = 512, 2048, 512, 256, 2048, 512
+FLOPS = 2 * K * H * S + 2 * K * H * S
+
+F32 = mybir.dt.float32
+BF16 = mybir.dt.bfloat16
+I32 = mybir.dt.int32
+U32 = mybir.dt.uint32
+U16 = mybir.dt.uint16
+U8 = mybir.dt.uint8
+FP8X4 = mybir.dt.float8_e4m3fn_x4
+COPY = mybir.ActivationFunctionType.Copy
+ALU = mybir.AluOpType
+
+P = 128
+PACK = 4
+HALF = S // 2
+SIXTEENTH = 0.0625
+PLANE_ORDER = (0, 2, 1, 3)
+
+
+def tile_picked_pqord_none_p_kernel(
+    tc, x_words, x_scales, d_words, d_scales, gs, offs, k1, la, lb, k2, out
+):
+    nc = tc.nc
+    with ExitStack() as ctx:
+        keep = ctx.enter_context(tc.tile_pool(name="keep", bufs=1))
+        ring = ctx.enter_context(tc.tile_pool(name="ring", bufs=2))
+        psum = ctx.enter_context(tc.psum_pool(name="psum", bufs=8))
+
+        k1_t = keep.tile([P, H // 16], U16, name="k1_t")
+        offs_t = keep.tile([P, S // 16], U16, name="offs_t")
+        k2_t = keep.tile([P, H // 16], U16, name="k2_t")
+        la_t = keep.tile([P, V // 16], U16, name="la_t")
+        lb_t = keep.tile([P, V // 16], U16, name="lb_t")
+        d_bytes = keep.tile([P, G], U8, name="d_bytes", align_bytes=64)
+        x_bytes = keep.tile([P, T], U8, name="x_bytes", tag="after_x_bytes", align_bytes=64)
+        d_table = keep.tile([P, G], U32, name="d_table", align_bytes=64)
+        x_table = keep.tile([P, T], U32, name="x_table", tag="after_x_words", align_bytes=64)
+        w2_scales = keep.tile([P, H], U8, name="w2_scales", align_bytes=64)
+
+        nc.vector.memset(x_bytes[:].bitcast(I32), 0)
+        nc.vector.memset(w2_scales[:].bitcast(I32), 0)
+        nc.sync.dma_start(k1_t[:], k1)
+        nc.sync.dma_start(
+            d_bytes[:].bitcast(I32), d_scales[0].bitcast(I32).unsqueeze(1).to_broadcast([16, 8, G // 4])
+        )
+        for tile, source in ((offs_t, offs), (k2_t, k2), (la_t, la), (lb_t, lb)):
+            nc.sync.dma_start(tile[:], source)
+        nc.sync.dma_start(d_table[:].bitcast(I32), d_words[0].rearrange("p n t -> p (n t)").bitcast(I32))
+        for q in range(4):
+            nc.scalar.dma_start(x_bytes[32 * q : 32 * q + 4, :].bitcast(I32), x_scales[0, 4 * q : 4 * q + 4, :].bitcast(I32))
+        nc.sync.dma_start(x_table[:].bitcast(I32), x_words[0].rearrange("p n t -> p (n t)").bitcast(I32))
+
+        w1_picked_bytes = keep.tile([P, H], U8, name="w1_picked_bytes", tag="picked", align_bytes=64)
+        w1_scales = keep.tile([P, H], U8, name="w1_scales", align_bytes=64)
+        nc.vector.tensor_copy(w1_picked_bytes[:], d_bytes[:].indirect(k1_t[:]))
+        nc.vector.tensor_copy(
+            w1_scales[:].rearrange("p (t c i) -> p c t i", t=PACK, i=16),
+            w1_picked_bytes[:].rearrange("p (c i t) -> p c t i", t=PACK, i=16),
+        )
+        for r in range(1, 4):
+            nc.scalar.dma_start(w1_scales[r:P:32, :].bitcast(I32), w1_scales[8 * r : P : 32, :].bitcast(I32))
+
+        w1_picked_words = keep.tile([P, H], U32, name="w1_picked_words", tag="picked", align_bytes=64)
+        w1_words = keep.tile([P, H], U32, name="w1_words", align_bytes=64)
+        nc.vector.tensor_copy(w1_picked_words[:], d_table[:].indirect(k1_t[:]))
+        nc.vector.tensor_copy(
+            w1_words[:].rearrange("p (t c i) -> p c t i", t=PACK, i=4),
+            w1_picked_words[:].rearrange("p (c i t) -> p c t i", t=PACK, i=4),
+        )
+
+        xq_scales = keep.tile([P, S], U8, name="xq_scales", tag="picked", align_bytes=64)
+        xq_words = keep.tile([P, S], U32, name="xq_words", align_bytes=64)
+        nc.vector.tensor_copy(xq_scales[:], x_bytes[:].indirect(offs_t[:]))
+        nc.vector.tensor_copy(xq_words[:], x_table[:].indirect(offs_t[:]))
+
+        gain = keep.tile([P, PACK], F32, name="gain", tag="after_x_bytes", align_bytes=64)
+        nc.sync.dma_start(gain[:], gs.rearrange("(p t) o -> p (t o)", t=PACK))
+
+        w2_picked_bytes = keep.tile([P, H], U8, name="w2_picked_bytes", align_bytes=64)
+        w2_words = keep.tile([P, H], U32, name="w2_words", tag="after_x_words", align_bytes=64)
+        nc.vector.tensor_copy(w2_picked_bytes[:], d_bytes[:].indirect(k2_t[:]))
+        nc.vector.tensor_copy(w2_words[:], d_table[:].indirect(k2_t[:]))
+        for r in range(4):
+            nc.sync.dma_start(w2_scales[r:P:32, :].bitcast(I32), w2_picked_bytes[8 * r : P : 32, :].bitcast(I32))
+
+        z_halves = [keep.tile([P, HALF, PACK], BF16, name=f"z_half{u}", align_bytes=64) for u in range(2)]
+        sides = {}
+        for t in PLANE_ORDER:
+            cols = slice(P * t, P * (t + 1))
+            acc = psum.tile([P, S], F32, name="acc")
+            nc.tensor.matmul_mx(
+                out=acc[:],
+                lhsT=w1_words[:, cols].bitcast(FP8X4),
+                lhsT_scale=w1_scales[:, cols],
+                rhs=xq_words[:].bitcast(FP8X4),
+                rhs_scale=xq_scales[:],
+                start=True,
+                stop=True,
+            )
+            h = keep.tile([P, S], F32, name=f"h{t}", align_bytes=64)
+            nc.scalar.activation(h[:], acc[:], COPY, scale=SIXTEENTH)
+            p_side = keep.tile([P, V], F32, name=f"p_side{t}", align_bytes=64)
+            q_side = keep.tile([P, V], F32, name=f"q_side{t}", align_bytes=64)
+            if t == PLANE_ORDER[0]:
+                nc.vector.tensor_copy(p_side[:], h[:].indirect(la_t[:]))
+            else:
+                nc.scalar.activation(p_side[:], h[:].indirect(la_t[:]), COPY)
+            nc.scalar.activation(q_side[:], h[:].indirect(lb_t[:]), COPY)
+            sides[t] = (p_side, q_side)
+
+        def compare(t):
+            p_side, q_side = sides[t]
+            hi = keep.tile([P, V], F32, name=f"hi{t}", align_bytes=64)
+            lo = keep.tile([P, V], F32, name=f"lo{t}", align_bytes=64)
+            nc.vector.tensor_tensor(hi[:], p_side[:], q_side[:], ALU.max)
+            nc.vector.tensor_tensor(lo[:], p_side[:], q_side[:], ALU.min)
+            return hi, lo
+
+        hi, lo = compare(PLANE_ORDER[0])
+        for n, t in enumerate(PLANE_ORDER):
+            ordered = ring.tile([P, S], F32, name="ordered", align_bytes=64)
+            nc.vector.tensor_copy(ordered[:].indirect(la_t[:]), hi[:])
+            lo_now = lo
+            if n + 1 < PACK:
+                hi, lo = compare(PLANE_ORDER[n + 1])
+            nc.vector.tensor_copy(ordered[:].indirect(lb_t[:]), lo_now[:])
+            for u in range(2):
+                places = slice(HALF * u, HALF * (u + 1))
+                if t == PLANE_ORDER[-1]:
+                    nc.vector.tensor_scalar(z_halves[u][:, :, t], ordered[:, places], gain[:, t : t + 1], None, ALU.mult)
+                else:
+                    nc.scalar.activation(z_halves[u][:, :, t], ordered[:, places], COPY, scale=gain[:, t : t + 1])
+
+        for u in range(2):
+            places = slice(HALF * u, HALF * (u + 1))
+            z_words = keep.tile([P, HALF], U32, name=f"z_words{u}", align_bytes=64)
+            z_scales = keep.tile([P, HALF], U8, name=f"z_scales{u}", align_bytes=64)
+            nc.vector.quantize_mx(
+                out=z_words[:].bitcast(FP8X4), scales=z_scales[:], in_=z_halves[u][:].rearrange("p n t -> p (n t)")
+            )
+            for b in range(H // P):
+                rows = slice(P * b, P * (b + 1))
+                acc = psum.tile([P, HALF], F32, name="acc")
+                nc.tensor.matmul_mx(
+                    out=acc[:],
+                    lhsT=w2_words[:, rows].bitcast(FP8X4),
+                    lhsT_scale=w2_scales[:, rows],
+                    rhs=z_words[:].bitcast(FP8X4),
+                    rhs_scale=z_scales[:],
+                    start=True,
+                    stop=True,
+                )
+                result = keep.tile([P, HALF], F32, name=f"result{u}_{b}", align_bytes=64)
+                if b % 2 == 0 or (u == 0 and b == 1):
+                    nc.scalar.activation(result[:], acc[:], COPY, scale=SIXTEENTH)
+                else:
+                    nc.vector.tensor_scalar(result[:], acc[:], SIXTEENTH, None, ALU.mult)
+                nc.sync.dma_start(out[rows, places], result[:])

@@ -29,6 +29,7 @@ def tile_picked_pqord_none_p_kernel(
     with ExitStack() as ctx:
         keep = ctx.enter_context(tc.tile_pool(name="keep", bufs=1))
         ring = ctx.enter_context(tc.tile_pool(name="ring", bufs=2))
+        shared = ctx.enter_context(tc.tile_pool(name="shared", bufs=1))
         psum = ctx.enter_context(tc.psum_pool(name="psum", bufs=8))
 
         k1_t = keep.tile([P, H // 16], U16, name="k1_t")
@@ -37,23 +38,26 @@ def tile_picked_pqord_none_p_kernel(
         la_t = keep.tile([P, V // 16], U16, name="la_t")
         lb_t = keep.tile([P, V // 16], U16, name="lb_t")
         d_bytes = keep.tile([P, G], U8, name="d_bytes", align_bytes=64)
-        x_bytes = keep.tile([P, T], U8, name="x_bytes", tag="after_x_bytes", align_bytes=64)
+        x_bytes = keep.tile([P, T], U8, name="x_bytes", align_bytes=64)
         d_table = keep.tile([P, G], U32, name="d_table", align_bytes=64)
-        x_table = keep.tile([P, T], U32, name="x_table", tag="after_x_words", align_bytes=64)
+        x_table = shared.tile([P, T], U32, name="x_table", align_bytes=64, offset=0)
         w2_scales = keep.tile([P, H], U8, name="w2_scales", align_bytes=64)
 
         nc.vector.memset(x_bytes[:].bitcast(I32), 0)
         nc.vector.memset(w2_scales[:].bitcast(I32), 0)
         nc.sync.dma_start(k1_t[:], k1)
-        nc.sync.dma_start(
+        nc.scalar.dma_start(
             d_bytes[:].bitcast(I32), d_scales[0].bitcast(I32).unsqueeze(1).to_broadcast([16, 8, G // 4])
         )
-        for tile, source in ((offs_t, offs), (k2_t, k2), (la_t, la), (lb_t, lb)):
-            nc.sync.dma_start(tile[:], source)
         nc.sync.dma_start(d_table[:].bitcast(I32), d_words[0].rearrange("p n t -> p (n t)").bitcast(I32))
+        nc.sync.dma_start(offs_t[:], offs)
         for q in range(4):
             nc.scalar.dma_start(x_bytes[32 * q : 32 * q + 4, :].bitcast(I32), x_scales[0, 4 * q : 4 * q + 4, :].bitcast(I32))
         nc.sync.dma_start(x_table[:].bitcast(I32), x_words[0].rearrange("p n t -> p (n t)").bitcast(I32))
+        for tile, source in ((k2_t, k2), (la_t, la), (lb_t, lb)):
+            nc.sync.dma_start(tile[:], source)
+        gain = keep.tile([P, PACK], F32, name="gain", align_bytes=64)
+        nc.sync.dma_start(gain[:], gs.rearrange("(p t) o -> p (t o)", t=PACK))
 
         w1_picked_bytes = keep.tile([P, H], U8, name="w1_picked_bytes", tag="picked", align_bytes=64)
         w1_scales = keep.tile([P, H], U8, name="w1_scales", align_bytes=64)
@@ -76,13 +80,13 @@ def tile_picked_pqord_none_p_kernel(
         xq_scales = keep.tile([P, S], U8, name="xq_scales", tag="picked", align_bytes=64)
         xq_words = keep.tile([P, S], U32, name="xq_words", align_bytes=64)
         nc.vector.tensor_copy(xq_scales[:], x_bytes[:].indirect(offs_t[:]))
-        nc.vector.tensor_copy(xq_words[:], x_table[:].indirect(offs_t[:]))
+        for u in range(2):
+            nc.vector.tensor_copy(
+                xq_words[:, HALF * u : HALF * (u + 1)], x_table[:].indirect(offs_t[:, 16 * u : 16 * (u + 1)])
+            )
 
-        gain = keep.tile([P, PACK], F32, name="gain", tag="after_x_bytes", align_bytes=64)
-        nc.sync.dma_start(gain[:], gs.rearrange("(p t) o -> p (t o)", t=PACK))
-
-        w2_picked_bytes = keep.tile([P, H], U8, name="w2_picked_bytes", align_bytes=64)
-        w2_words = keep.tile([P, H], U32, name="w2_words", tag="after_x_words", align_bytes=64)
+        w2_picked_bytes = shared.tile([P, H], U8, name="w2_picked_bytes", align_bytes=64, offset=4 * H)
+        w2_words = shared.tile([P, H], U32, name="w2_words", align_bytes=64, offset=0)
         nc.vector.tensor_copy(w2_picked_bytes[:], d_bytes[:].indirect(k2_t[:]))
         nc.vector.tensor_copy(w2_words[:], d_table[:].indirect(k2_t[:]))
         for r in range(4):
@@ -92,24 +96,24 @@ def tile_picked_pqord_none_p_kernel(
         sides = {}
         for t in PLANE_ORDER:
             cols = slice(P * t, P * (t + 1))
-            acc = psum.tile([P, S], F32, name="acc")
-            nc.tensor.matmul_mx(
-                out=acc[:],
-                lhsT=w1_words[:, cols].bitcast(FP8X4),
-                lhsT_scale=w1_scales[:, cols],
-                rhs=xq_words[:].bitcast(FP8X4),
-                rhs_scale=xq_scales[:],
-                start=True,
-                stop=True,
-            )
-            h = keep.tile([P, S], F32, name=f"h{t}", align_bytes=64)
-            nc.scalar.activation(h[:], acc[:], COPY, scale=SIXTEENTH)
+            h = keep.tile([P, S], F32, name="h", align_bytes=64)
+            width = HALF if t == PLANE_ORDER[0] else S
+            for start in range(0, S, width):
+                places = slice(start, start + width)
+                acc = psum.tile([P, width], F32, name="acc")
+                nc.tensor.matmul_mx(
+                    out=acc[:],
+                    lhsT=w1_words[:, cols].bitcast(FP8X4),
+                    lhsT_scale=w1_scales[:, cols],
+                    rhs=xq_words[:, places].bitcast(FP8X4),
+                    rhs_scale=xq_scales[:, places],
+                    start=True,
+                    stop=True,
+                )
+                nc.scalar.activation(h[:, places], acc[:], COPY, scale=SIXTEENTH)
             p_side = keep.tile([P, V], F32, name=f"p_side{t}", align_bytes=64)
             q_side = keep.tile([P, V], F32, name=f"q_side{t}", align_bytes=64)
-            if t == PLANE_ORDER[0]:
-                nc.vector.tensor_copy(p_side[:], h[:].indirect(la_t[:]))
-            else:
-                nc.scalar.activation(p_side[:], h[:].indirect(la_t[:]), COPY)
+            nc.scalar.activation(p_side[:], h[:].indirect(la_t[:]), COPY)
             nc.scalar.activation(q_side[:], h[:].indirect(lb_t[:]), COPY)
             sides[t] = (p_side, q_side)
 
@@ -131,7 +135,7 @@ def tile_picked_pqord_none_p_kernel(
             nc.vector.tensor_copy(ordered[:].indirect(lb_t[:]), lo_now[:])
             for u in range(2):
                 places = slice(HALF * u, HALF * (u + 1))
-                if t == PLANE_ORDER[-1]:
+                if t == PLANE_ORDER[-1] and u == 0:
                     nc.vector.tensor_scalar(z_halves[u][:, :, t], ordered[:, places], gain[:, t : t + 1], None, ALU.mult)
                 else:
                     nc.scalar.activation(z_halves[u][:, :, t], ordered[:, places], COPY, scale=gain[:, t : t + 1])

from contextlib import ExitStack

import concourse.mybir as mybir

K, T, S, V, G, H = 512, 2048, 512, 256, 2048, 512
FLOPS = 2 * K * H * S + 2 * K * H * S

F32 = mybir.dt.float32
BF16 = mybir.dt.bfloat16
I32 = mybir.dt.int32
U32 = mybir.dt.uint32
U16 = mybir.dt.uint16
U8 = mybir.dt.uint8
FP8X4 = mybir.dt.float8_e4m3fn_x4
COPY = mybir.ActivationFunctionType.Copy
ALU = mybir.AluOpType

P = 128
PACK = 4
HALF = S // 2
SIXTEENTH = 0.0625
PLANE_ORDER = (0, 2, 1, 3)


def tile_picked_pqord_none_p_kernel(
    tc, x_words, x_scales, d_words, d_scales, gs, offs, k1, la, lb, k2, out
):
    nc = tc.nc
    with ExitStack() as ctx:
        keep = ctx.enter_context(tc.tile_pool(name="keep", bufs=1))
        ring = ctx.enter_context(tc.tile_pool(name="ring", bufs=2))
        shared = ctx.enter_context(tc.tile_pool(name="shared", bufs=1))
        psum = ctx.enter_context(tc.psum_pool(name="psum", bufs=8))

        k1_t = keep.tile([P, H // 16], U16, name="k1_t")
        offs_t = keep.tile([P, S // 16], U16, name="offs_t")
        k2_t = keep.tile([P, H // 16], U16, name="k2_t")
        la_t = keep.tile([P, V // 16], U16, name="la_t")
        lb_t = keep.tile([P, V // 16], U16, name="lb_t")
        d_bytes = keep.tile([P, G], U8, name="d_bytes", align_bytes=64)
        x_bytes = keep.tile([P, T], U8, name="x_bytes", align_bytes=64)
        d_table = keep.tile([P, G], U32, name="d_table", align_bytes=64)
        x_table = shared.tile([P, T], U32, name="x_table", align_bytes=64, offset=0)
        w2_scales = keep.tile([P, H], U8, name="w2_scales", align_bytes=64)

        nc.vector.memset(x_bytes[:].bitcast(I32), 0)
        nc.vector.memset(w2_scales[:].bitcast(I32), 0)
        nc.sync.dma_start(k1_t[:], k1)
        nc.scalar.dma_start(
            d_bytes[:].bitcast(I32), d_scales[0].bitcast(I32).unsqueeze(1).to_broadcast([16, 8, G // 4])
        )
        nc.sync.dma_start(d_table[:].bitcast(I32), d_words[0].rearrange("p n t -> p (n t)").bitcast(I32))
        nc.sync.dma_start(offs_t[:], offs)
        for q in range(4):
            nc.scalar.dma_start(x_bytes[32 * q : 32 * q + 4, :].bitcast(I32), x_scales[0, 4 * q : 4 * q + 4, :].bitcast(I32))
        nc.sync.dma_start(x_table[:].bitcast(I32), x_words[0].rearrange("p n t -> p (n t)").bitcast(I32))
        for tile, source in ((k2_t, k2), (la_t, la), (lb_t, lb)):
            nc.sync.dma_start(tile[:], source)
        gain = keep.tile([P, PACK], F32, name="gain", align_bytes=64)
        nc.sync.dma_start(gain[:], gs.rearrange("(p t) o -> p (t o)", t=PACK))

        w1_picked_bytes = keep.tile([P, H], U8, name="w1_picked_bytes", tag="picked", align_bytes=64)
        w1_scales = keep.tile([P, H], U8, name="w1_scales", align_bytes=64)
        nc.vector.tensor_copy(w1_picked_bytes[:], d_bytes[:].indirect(k1_t[:]))
        nc.vector.tensor_copy(
            w1_scales[:].rearrange("p (t c i) -> p c t i", t=PACK, i=16),
            w1_picked_bytes[:].rearrange("p (c i t) -> p c t i", t=PACK, i=16),
        )
        for r in range(1, 4):
            nc.scalar.dma_start(w1_scales[r:P:32, :].bitcast(I32), w1_scales[8 * r : P : 32, :].bitcast(I32))

        w1_picked_words = keep.tile([P, H], U32, name="w1_picked_words", tag="picked", align_bytes=64)
        w1_words = keep.tile([P, H], U32, name="w1_words", align_bytes=64)
        nc.vector.tensor_copy(w1_picked_words[:], d_table[:].indirect(k1_t[:]))
        nc.vector.tensor_copy(
            w1_words[:].rearrange("p (t c i) -> p c t i", t=PACK, i=4),
            w1_picked_words[:].rearrange("p (c i t) -> p c t i", t=PACK, i=4),
        )

        xq_scales = keep.tile([P, S], U8, name="xq_scales", tag="picked", align_bytes=64)
        xq_words = keep.tile([P, S], U32, name="xq_words", align_bytes=64)
        nc.vector.tensor_copy(xq_scales[:], x_bytes[:].indirect(offs_t[:]))
        for u in range(2):
            nc.vector.tensor_copy(
                xq_words[:, HALF * u : HALF * (u + 1)], x_table[:].indirect(offs_t[:, 16 * u : 16 * (u + 1)])
            )

        w2_picked_bytes = shared.tile([P, H], U8, name="w2_picked_bytes", align_bytes=64, offset=4 * H)
        w2_words = shared.tile([P, H], U32, name="w2_words", align_bytes=64, offset=0)
        nc.vector.tensor_copy(w2_picked_bytes[:], d_bytes[:].indirect(k2_t[:]))
        nc.vector.tensor_copy(w2_words[:], d_table[:].indirect(k2_t[:]))
        for r in range(4):
            nc.sync.dma_start(w2_scales[r:P:32, :].bitcast(I32), w2_picked_bytes[8 * r : P : 32, :].bitcast(I32))

        z_halves = [keep.tile([P, HALF, PACK], BF16, name=f"z_half{u}", align_bytes=64) for u in range(2)]
        sides = {}
        for t in PLANE_ORDER:
            cols = slice(P * t, P * (t + 1))
            h = keep.tile([P, S], F32, name="h", align_bytes=64)
            width = HALF if t == PLANE_ORDER[0] else S
            for start in range(0, S, width):
                places = slice(start, start + width)
                acc = psum.tile([P, width], F32, name="acc")
                nc.tensor.matmul_mx(
                    out=acc[:],
                    lhsT=w1_words[:, cols].bitcast(FP8X4),
                    lhsT_scale=w1_scales[:, cols],
                    rhs=xq_words[:, places].bitcast(FP8X4),
                    rhs_scale=xq_scales[:, places],
                    start=True,
                    stop=True,
                )
                nc.scalar.activation(h[:, places], acc[:], COPY, scale=SIXTEENTH)
            p_side = keep.tile([P, V], F32, name=f"p_side{t}", align_bytes=64)
            q_side = keep.tile([P, V], F32, name=f"q_side{t}", align_bytes=64)
            nc.scalar.activation(p_side[:], h[:].indirect(la_t[:]), COPY)
            nc.scalar.activation(q_side[:], h[:].indirect(lb_t[:]), COPY)
            sides[t] = (p_side, q_side)

        def compare(t):
            p_side, q_side = sides[t]
            hi = keep.tile([P, V], F32, name=f"hi{t}", align_bytes=64)
            lo = keep.tile([P, V], F32, name=f"lo{t}", align_bytes=64)
            nc.vector.tensor_tensor(hi[:], p_side[:], q_side[:], ALU.max)
            nc.vector.tensor_tensor(lo[:], p_side[:], q_side[:], ALU.min)
            return hi, lo

        hi, lo = compare(PLANE_ORDER[0])
        for n, t in enumerate(PLANE_ORDER):
            ordered = ring.tile([P, S], F32, name="ordered", align_bytes=64)
            nc.vector.tensor_copy(ordered[:].indirect(la_t[:]), hi[:])
            lo_now = lo
            if n + 1 < PACK:
                hi, lo = compare(PLANE_ORDER[n + 1])
            nc.vector.tensor_copy(ordered[:].indirect(lb_t[:]), lo_now[:])
            for u in range(2):
                places = slice(HALF * u, HALF * (u + 1))
                if t == PLANE_ORDER[-1] and u == 0:
                    nc.vector.tensor_scalar(z_halves[u][:, :, t], ordered[:, places], gain[:, t : t + 1], None, ALU.mult)
                else:
                    nc.scalar.activation(z_halves[u][:, :, t], ordered[:, places], COPY, scale=gain[:, t : t + 1])

        for u in range(2):
            places = slice(HALF * u, HALF * (u + 1))
            z_words = keep.tile([P, HALF], U32, name=f"z_words{u}", align_bytes=64)
            z_scales = keep.tile([P, HALF], U8, name=f"z_scales{u}", align_bytes=64)
            nc.vector.quantize_mx(
                out=z_words[:].bitcast(FP8X4), scales=z_scales[:], in_=z_halves[u][:].rearrange("p n t -> p (n t)")
            )
            for b in range(H // P):
                rows = slice(P * b, P * (b + 1))
                acc = psum.tile([P, HALF], F32, name="acc")
                nc.tensor.matmul_mx(
                    out=acc[:],
                    lhsT=w2_words[:, rows].bitcast(FP8X4),
                    lhsT_scale=w2_scales[:, rows],
                    rhs=z_words[:].bitcast(FP8X4),
                    rhs_scale=z_scales[:],
                    start=True,
                    stop=True,
                )
                result = keep.tile([P, HALF], F32, name=f"result{u}_{b}", align_bytes=64)
                if b % 2 == 0 or (u == 0 and b == 1):
                    nc.scalar.activation(result[:], acc[:], COPY, scale=SIXTEENTH)
                else:
                    nc.vector.tensor_scalar(result[:], acc[:], SIXTEENTH, None, ALU.mult)
                nc.sync.dma_start(out[rows, places], result[:])
